import numpy as np
import ml_dtypes


def mxq(x, axis, fmt="e4m3"):
    dtype, down = {"e4m3": (ml_dtypes.float8_e4m3fn, 7), "e5m2": (ml_dtypes.float8_e5m2, 14)}[fmt]
    v = np.moveaxis(np.asarray(x, np.float32).astype(ml_dtypes.bfloat16).astype(np.float64), axis, -1)
    blocks = v.reshape(v.shape[:-1] + (-1, 32))
    amax = np.abs(blocks).max(-1, keepdims=True)
    byte = np.maximum(np.where(amax > 0, np.frexp(amax)[1] - 1 + 127, 0) - down, 1)
    scale = np.exp2(byte - 127.0)
    codes = (blocks / scale).astype(np.float32).astype(dtype).astype(np.float64)
    return np.moveaxis((codes * scale).reshape(v.shape), -1, axis)


WIDE = False


def mx_kscale(k):
    if not WIDE:
        return np.ones(k)
    levels = np.array([10, -10, 5, -5, 0])
    if k % 512:
        return np.exp2(np.random.permutation(np.resize(levels, k // 32))).repeat(32)
    a = np.empty((k // 512, 16))
    for p in range(k // 512):
        a[p, :8] = np.random.permutation(np.resize(levels, 8))
        for g in range(8):
            far = levels[np.abs(levels - a[p, g]) >= 10]
            a[p, g + 8] = far[np.random.randint(len(far))]
    return np.exp2(a.ravel()).repeat(32)


def f64(x):
    return np.asarray(x).astype(np.float64)


def striped(idx):
    return np.tile(idx.reshape(-1, 16).T, (8, 1)).astype(np.uint16)


def unstriped(offs):
    return offs[:16].T.reshape(-1).astype(np.int64)


E2M1 = np.array([0.0, 0.5, 1.0, 1.5, 2.0, 3.0, 4.0, 6.0, -0.0, -0.5, -1.0, -1.5, -2.0, -3.0, -4.0, -6.0])


def pack_weight(w, fmt):
    k, n = w.shape
    w = f64(np.asarray(w, np.float32).astype(ml_dtypes.bfloat16)).reshape(k // 32, 32, n)
    amax = np.abs(w).max(1)
    if fmt == "e4m3":
        byte = np.frexp(amax)[1] - 1 + 127 - 7
    else:
        mant, ex = np.frexp(amax / 6.0)
        byte = np.where(mant > 0.5, ex, ex - 1) + 127
    byte = np.clip(np.where(amax > 0, byte, 1), 1, 254)
    scaled = (w * np.exp2(127.0 - byte)[:, None, :]).reshape(k, n).astype(np.float32)
    by_word = np.ascontiguousarray(scaled.reshape(k // 512, 128, 4, n).transpose(0, 1, 3, 2))
    if fmt == "e4m3":
        words = by_word.astype(ml_dtypes.float8_e4m3fn).view(np.uint8)
    else:
        c = by_word.astype(ml_dtypes.float4_e2m1fn).view(np.uint8) & 0xF
        words = (c[..., 0::2] | (c[..., 1::2] << 4)).reshape(k // 512, 128, 2 * n)
    return np.ascontiguousarray(words), np.ascontiguousarray(byte.astype(np.uint8).reshape(k // 512, 16, n))


def unpack_weight(words, scales, fmt):
    g, _, n = scales.shape
    words = np.ascontiguousarray(words).reshape(g, 128, n, -1)
    if fmt == "e4m3":
        vals = words.view(ml_dtypes.float8_e4m3fn).astype(np.float64)
    else:
        nib = np.empty((g, 128, n, 4), np.uint8)
        nib[..., 0::2] = words & 0xF
        nib[..., 1::2] = words >> 4
        vals = E2M1[nib]
    vals = vals * np.repeat(np.exp2(scales.astype(np.float64) - 127.0), 8, axis=1)[..., None]
    return vals.transpose(0, 1, 3, 2).reshape(g * 512, n)


def gelu(v):
    return 0.5 * v * (1.0 + np.tanh(np.sqrt(2.0 / np.pi) * (v + 0.044715 * v**3)))


K, H, N, T, TG, S, T2 = 1024, 1024, 512, 2048, 1024, 512, 1024

def setup_inputs():
    n = np.random.standard_normal
    s = mx_kscale(K)[:, None]
    u = mx_kscale(H)[:, None]
    tab_words, tab_scales = pack_weight(n((K, T)) * s, "e4m3")
    tab2_words, tab2_scales = pack_weight(n((K, TG)) * s, "e4m3")
    w1_words, w1_scales = pack_weight(n((K, H)) / np.sqrt(K) / s * u.T, "e2m1")
    return {
        "tab_words": tab_words, "tab_scales": tab_scales,
        "tab2_words": tab2_words, "tab2_scales": tab2_scales,
        "offs": striped(np.random.permutation(T)[:S]),
        "offs2": striped(np.random.permutation(TG)[:S]),
        "offs3": striped(np.random.permutation(T2)[:S]),
        "offs4": striped(np.random.permutation(T2)[:S]),
        "w1_words": w1_words, "w1_scales": w1_scales,
        "base": (0.7 * n(H) * u[:, 0]).astype(np.float32),
        "w2": (0.55 * n((K, H)) / np.sqrt(K) / s).astype(np.float32),
        "amp": (1.3 * n(H) * u[:, 0]).astype(np.float32),
        "wg1": np.exp(0.3 * n((128, S))).astype(np.float32),
        "wg2": np.exp(0.3 * n((128, S))).astype(np.float32),
        "ephem": (0.8 * n((H, T2)) * u).astype(np.float32),
        "w3": (n((H, N)) / np.sqrt(H) / u).astype(np.float32),
    }

def reference(tab_words, tab_scales, tab2_words, tab2_scales, offs, offs2, offs3, offs4,
              w1_words, w1_scales, base, w2, amp, wg1, wg2, ephem, w3):
    v = unpack_weight(tab_words, tab_scales, "e4m3")[:, unstriped(offs)]
    v2 = unpack_weight(tab2_words, tab2_scales, "e4m3")[:, unstriped(offs2)]
    w1 = unpack_weight(w1_words, w1_scales, "e2m1")
    h1 = np.maximum(w1.T @ v, f64(base)[:, None])
    h2 = f64(amp)[:, None] * np.cos(mxq(f64(w2), 0, "e4m3").T @ v2)
    pa = np.zeros((H, T2))
    pa[:, unstriped(offs3)] = np.tile(f64(wg1), (H // 128, 1)) * h1
    pb = np.zeros((H, T2))
    pb[:, unstriped(offs4)] = np.tile(f64(wg2), (H // 128, 1)) * h2
    z = np.maximum(pa + pb, f64(ephem))
    y = mxq(f64(w3), 0, "e4m3").T @ mxq(z, 0, "e4m3")
    return y * np.tanh(y)

@@ -1,0 +1,342 @@
+import math
+from contextlib import ExitStack
+
+import concourse.mybir as mybir
+from concourse.masks import make_identity
+
+K, H, N, T, TG, S, T2 = 1024, 1024, 512, 2048, 1024, 512, 1024
+FLOPS = 2 * K * H * S * 2 + 2 * H * N * T2
+
+F32 = mybir.dt.float32
+BF16 = mybir.dt.bfloat16
+I32 = mybir.dt.int32
+U32 = mybir.dt.uint32
+U16 = mybir.dt.uint16
+U8 = mybir.dt.uint8
+FP8X4 = mybir.dt.float8_e4m3fn_x4
+FP4X4 = mybir.dt.float4_e2m1fn_x4
+ACT = mybir.ActivationFunctionType
+ALU = mybir.AluOpType
+
+P = 128
+PASS = 512
+SLICES = H // P
+PAGES_B = 3
+ROUND_BIAS = 0.0
+
+
+def tile_list_lightcurve_slot_scores_kernel(
+    tc, tab_words, tab_scales, tab2_words, tab2_scales, offs, offs2, offs3, offs4,
+    w1_words, w1_scales, base, w2, amp, wg1, wg2, ephem, w3, out,
+):
+    nc = tc.nc
+    with ExitStack() as ctx:
+        lists = ctx.enter_context(tc.tile_pool(name="lists", bufs=1))
+        keep = ctx.enter_context(tc.tile_pool(name="keep", bufs=1))
+        ring = ctx.enter_context(tc.tile_pool(name="ring", bufs=2))
+        psum = ctx.enter_context(tc.psum_pool(name="psum", bufs=2))
+
+        def wide(shape, dtype, name, slot):
+            return keep.tile(shape, dtype, name=name, tag=f"wide{slot}", align_bytes=64)
+
+        def stage(shape, dtype, name):
+            return ring.tile(shape, dtype, name=name, tag="stage", bufs=2, align_bytes=64)
+
+        def feat(name):
+            return ring.tile([P, S], F32, name=name, tag="feat", bufs=SLICES)
+
+        def load_list(src, name):
+            t = lists.tile([P, S // 16], U16, name=name)
+            nc.sync.dma_start(t[:], src)
+            return t
+
+        def load_scales_side_by_side(src, width, name, clear, queue):
+            t = keep.tile([P, 2 * width], U8, name=name, tag=name, align_bytes=64)
+            view = t[:].bitcast(I32)
+            clear.memset(view, 0)
+            rows = src.bitcast(I32)
+            for q in range(4):
+                queue.dma_start(
+                    view[32 * q : 32 * q + 4, :].rearrange("r (a n) -> r a n", a=2),
+                    rows[:, 4 * q : 4 * q + 4, :].rearrange("a r n -> r a n"),
+                )
+            return t
+
+        tab_s = load_scales_side_by_side(tab_scales, T, "tab_s", nc.vector, nc.scalar)
+        list1 = load_list(offs, "list1")
+        list3 = load_list(offs3, "list3")
+        list2 = load_list(offs2, "list2")
+        list4 = load_list(offs4, "list4")
+        tab_w = []
+        for a in range(2):
+            t = wide([P, T], U32, f"tab_w{a}", a)
+            nc.sync.dma_start(t[:].bitcast(I32), tab_words[a].rearrange("p t i -> p (t i)").bitcast(I32))
+            tab_w.append(t)
+        tab2_w = wide([P, 2 * TG], U32, "tab2_w", 2)
+        nc.sync.dma_start(
+            tab2_w[:].bitcast(I32).rearrange("p (a t) -> p a t", a=2),
+            tab2_words.rearrange("a p t i -> p a (t i)").bitcast(I32),
+        )
+        w1_w = keep.tile([P, 2, 2 * H], U8, name="w1_w", align_bytes=64)
+        nc.sync.dma_start(
+            w1_w[:].rearrange("p a n -> p (a n)").bitcast(I32).rearrange("p (a n) -> p a n", a=2),
+            w1_words.bitcast(I32).rearrange("a p n -> p a n"),
+        )
+        w1_s = load_scales_side_by_side(w1_scales, H, "w1_s", nc.gpsimd, nc.gpsimd)
+        vec_rows = keep.tile([P, P], F32, name="vec_rows", tag="vec_rows", align_bytes=64)
+        nc.vector.memset(vec_rows[:], 0.0)
+        nc.gpsimd.dma_start(vec_rows[0:SLICES, :], base.rearrange("(s p) -> s p", p=P))
+        nc.gpsimd.dma_start(vec_rows[32 : 32 + SLICES, :], amp.rearrange("(s p) -> s p", p=P))
+        wg1_sb = keep.tile([P, S], F32, name="wg1_sb")
+        nc.sync.dma_start(wg1_sb[:], wg1)
+
+
+        tab2_s = keep.tile([P, TG], U8, name="tab2_s", align_bytes=64)
+        nc.vector.memset(tab2_s[:].bitcast(I32), 0)
+        for q in range(4):
+            nc.gpsimd.dma_start(
+                tab2_s[:].bitcast(I32)[32 * q : 32 * q + 8, :],
+                tab2_scales.bitcast(I32)[:, 4 * q : 4 * q + 4, :],
+            )
+
+        ident = keep.tile([P, P], F32, name="ident")
+        make_identity(nc, ident[:])
+        vec_ps = psum.tile([P, PASS], F32, name="vec_ps", tag="work", bufs=4)
+        nc.tensor.transpose(vec_ps[:, 0:P], vec_rows[:], ident[:])
+        vec = keep.tile([P, 64], F32, name="vec")
+        nc.scalar.copy(vec[:], vec_ps[:, 0:64])
+
+        page_a = [keep.tile([P, T2], F32, name=f"page_a{i}") for i in range(SLICES)]
+        page_b = [keep.tile([P, T2], F32, name=f"page_b{i}") for i in range(PAGES_B)]
+        for page in page_a + page_b:
+            nc.gpsimd.memset(page[:], 0.0)
+
+        v_w, v_s = [], []
+        for a in range(2):
+            s_t = keep.tile([P, S], U8, name=f"v_s{a}", align_bytes=64)
+            nc.vector.tensor_copy(s_t[:], tab_s[:, a * T : (a + 1) * T].indirect(list1[:]))
+            v_s.append(s_t)
+        v_both = keep.tile([P, 2, S], U32, name="v_both", tag="tab_s", align_bytes=64)
+        for a in range(2):
+            nc.vector.tensor_copy(v_both[:, a, :], tab_w[a][:].indirect(list1[:]))
+            v_w.append(v_both[:, a, :])
+
+
+        h1_raw = {}
+
+        def first_product(s):
+            acc = psum.tile([P, S], F32, name="acc", tag="mx")
+            for a in range(2):
+                nc.tensor.matmul_mx(
+                    out=acc[:],
+                    lhsT=w1_w[:, a, 2 * P * s : 2 * P * (s + 1)].bitcast(FP4X4),
+                    lhsT_scale=w1_s[:, a * H + P * s : a * H + P * (s + 1)],
+                    rhs=v_w[a][:].bitcast(FP8X4),
+                    rhs_scale=v_s[a][:],
+                    start=(a == 0),
+                    stop=(a == 1),
+                )
+            t = feat("h1_raw")
+            nc.scalar.copy(t[:], acc[:])
+            h1_raw[s] = t
+
+        def place_a(s):
+            h1 = keep.tile([P, S], F32, name="h1", tag=f"h1_{s}" if s < 2 else f"pre{min(s - 2, 2 + s % 2)}", align_bytes=64)
+            nc.vector.tensor_scalar(h1[:], h1_raw[s][:], vec[:, s : s + 1], None, ALU.max)
+            nc.vector.tensor_tensor(page_a[s][:].indirect(list3[:]), h1[:], wg1_sb[:], ALU.mult)
+
+        def load_rows(src, row0, col0, name, slot):
+            t = wide([P, 4, PASS], F32, name, slot)
+            nc.sync.dma_start(
+                t[:], src[row0 : row0 + PASS, col0 : col0 + PASS].rearrange("(p j) c -> p j c", j=4)
+            )
+            return t
+
+        def quantise_weight(raw, name, grouped):
+            nc.scalar.copy(
+                grouped[:].rearrange("p (c i) t -> p c t i", i=4),
+                raw[:].rearrange("p t (c i) -> p c t i", i=4),
+            )
+            codes = keep.tile([P, PASS], U32, name=name + "_w", align_bytes=64)
+            scales = keep.tile([P, PASS], U8, name=name + "_s", align_bytes=64)
+            nc.vector.quantize_mx(
+                out=codes[:].bitcast(FP8X4), scales=scales[:], in_=grouped[:].rearrange("p c t -> p (c t)")
+            )
+            return codes, scales
+
+        for s in range(SLICES):
+            first_product(s)
+
+        v2_w = []
+        v2_s = keep.tile([P, S], U8, name="v2_s", tag="vec_rows", align_bytes=64)
+        v2_both = wide([P, 2, S], U32, "v2_both", 1)
+        for a in range(2):
+            nc.vector.tensor_copy(v2_both[:, a, :], tab2_w[:, a * TG : (a + 1) * TG].indirect(list2[:]))
+            v2_w.append(v2_both[:, a, :])
+        nc.vector.tensor_copy(v2_s[:], tab2_s[:].indirect(list2[:]))
+
+        w2_raw = {}
+        for half in range(2):
+            for a in range(2):
+                w2_raw[a, half] = load_rows(w2, a * PASS, half * PASS, "w2_raw", ((3, 4), (0, 5))[half][a])
+            if half == 0:
+                wg2_sb = keep.tile([P, S], F32, name="wg2_sb")
+                nc.sync.dma_start(wg2_sb[:], wg2)
+        w3_raw = {0: load_rows(w3, 0, 0, "w3_raw", 2)}
+        eph = {}
+        for b, half, slot in ((0, 0, 6), (0, 1, 7)):
+            eph[b, half] = load_rows(ephem, b * PASS, half * PASS, "eph", slot)
+
+
+        w2_q = {}
+        cosine = {}
+
+        def quantise_w2(a, half):
+            w2_q[a, half] = quantise_weight(
+                w2_raw[a, half], f"w2_{a}{half}",
+                keep.tile([P, PASS, 4], BF16, name="grouped", tag=f"pre{2 * half + a}", align_bytes=64),
+            )
+
+        def second_product(s):
+            half, c0 = s // 4, (s % 4) * P
+            acc = psum.tile([P, S], F32, name="acc", tag="mx")
+            for a in range(2):
+                codes, scales = w2_q[a, half]
+                nc.tensor.matmul_mx(
+                    out=acc[:],
+                    lhsT=codes[:, c0 : c0 + P].bitcast(FP8X4),
+                    lhsT_scale=scales[:, c0 : c0 + P],
+                    rhs=v2_w[a][:].bitcast(FP8X4),
+                    rhs_scale=v2_s[4 * a : P, :],
+                    start=(a == 0),
+                    stop=(a == 1),
+                )
+            size = ring.tile([P, S], F32, name="size")
+            nc.scalar.activation(size[:], acc[:], ACT.Abs)
+            turns = ring.tile([P, S], U32, name="turns")
+            nc.scalar.activation(turns[:], size[:], ACT.Copy, bias=ROUND_BIAS, scale=1.0 / (2.0 * math.pi))
+            whole = ring.tile([P, S], F32, name="whole")
+            nc.scalar.activation(whole[:], turns[:], ACT.Copy, bias=0.0, scale=-2.0 * math.pi)
+            angle = psum.tile([P, 4, P], F32, name="angle", tag="work", bufs=4)
+            for blk in range(4):
+                cols = slice(blk * P, (blk + 1) * P)
+                nc.tensor.matmul(angle[:, blk, :], size[:, cols], ident[:], start=True, stop=False, is_transpose=True)
+                nc.tensor.matmul(angle[:, blk, :], whole[:, cols], ident[:], start=False, stop=True, is_transpose=True)
+            folded = ring.tile([P, 4, P], F32, name="folded")
+            nc.scalar.activation(folded[:], angle[:], ACT.Abs)
+            upright = psum.tile([P, S], F32, name="upright", tag="work", bufs=4)
+            for blk in range(4):
+                nc.tensor.transpose(upright[:, blk * P : (blk + 1) * P], folded[:, blk, :], ident[:])
+            c = keep.tile([P, S], F32, name="cos_last", tag="pre0", align_bytes=64) if s == SLICES - 1 else feat("cos_t")
+            nc.scalar.activation(c[:], upright[:], ACT.Sin, bias=math.pi / 2.0, scale=-1.0)
+            nc.scalar.activation(c[:], c[:], ACT.Copy, bias=0.0, scale=vec[:, 32 + s : 33 + s])
+            cosine[s] = c
+
+        turned = {}
+
+        def place_b(s):
+            pa, pb = page_a[s], page_b[s % PAGES_B]
+            nc.vector.tensor_tensor(pb[:].indirect(list4[:]), cosine[s][:], wg2_sb[:], ALU.mult)
+            b, sl = s // 4, s % 4
+            for half in range(2):
+                if sl == 0:
+                    turned[b, half] = wide([P, 4, 4, P], F32, "turned", ((0, 2), (3, 1))[b][half])
+                bank = psum.tile([P, 4, P], F32, name="sum_ps", tag="work", bufs=4)
+                for k, page in enumerate((pa, pb)):
+                    for blk in range(4):
+                        cols = slice(half * PASS + blk * P, half * PASS + (blk + 1) * P)
+                        nc.tensor.matmul(
+                            bank[:, blk, :], page[:, cols], ident[:],
+                            start=(k == 0 and blk == 0), stop=(k == 1 and blk == 3), is_transpose=True,
+                        )
+                nc.scalar.copy(
+                    turned[b, half][:, :, :, 32 * sl : 32 * (sl + 1)],
+                    bank[:].rearrange("p blk (q t) -> p blk t q", t=4),
+                )
+
+        z_q = {}
+
+        back = {}
+
+        def turn_back(b, half):
+            for blk in range(4):
+                bank = psum.tile([P, 4, P], F32, name="back_ps", tag=("turn", "mx")[blk % 2])
+                for t in range(4):
+                    nc.tensor.transpose(bank[:, t, :], turned[b, half][:, blk, t, :], ident[:])
+                back[b, half, blk] = bank
+
+        def make_z(b, half, z_bf):
+            for blk in range(4):
+                bank = back[b, half, blk]
+                nc.vector.tensor_tensor(
+                    z_bf[:, blk * P : (blk + 1) * P, :].rearrange("p (c i) t -> p c t i", i=4),
+                    bank[:].rearrange("p t (c i) -> p c t i", i=4),
+                    eph[b, half][:, :, blk * P : (blk + 1) * P].rearrange("p t (c i) -> p c t i", i=4),
+                    ALU.max,
+                )
+            codes = keep.tile([P, PASS], U32, name=f"z_w{b}{half}", align_bytes=64)
+            scales = keep.tile([P, PASS], U8, name=f"z_s{b}{half}", align_bytes=64)
+            nc.vector.quantize_mx(
+                out=codes[:].bitcast(FP8X4), scales=scales[:], in_=z_bf[:].rearrange("p c t -> p (c t)")
+            )
+            z_q[b, half] = (codes, scales)
+
+        def z_tile():
+            return ring.tile([P, PASS, 4], BF16, name="z_bf", align_bytes=64)
+
+        w3_q = {}
+
+        def quantise_w3(b):
+            w3_q[b] = quantise_weight(w3_raw[b], f"w3_{b}", z_tile())
+
+        def last_product(half, nb):
+            acc = psum.tile([P, PASS], F32, name="acc", tag="work", bufs=4)
+            for b in range(2):
+                nc.tensor.matmul_mx(
+                    out=acc[:],
+                    lhsT=w3_q[b][0][:, nb * P : (nb + 1) * P].bitcast(FP8X4),
+                    lhsT_scale=w3_q[b][1][:, nb * P : (nb + 1) * P],
+                    rhs=z_q[b, half][0][:].bitcast(FP8X4),
+                    rhs_scale=z_q[b, half][1][:],
+                    start=(b == 0),
+                    stop=(b == 1),
+                )
+            th = ring.tile([P, PASS], F32, name="th", bufs=4)
+            nc.scalar.activation(th[:], acc[:], ACT.Tanh)
+            res = feat("res")
+            nc.vector.tensor_tensor(res[:], acc[:], th[:], ALU.mult)
+            nc.sync.dma_start(out[nb * P : (nb + 1) * P, half * PASS : (half + 1) * PASS], res[:])
+
+        place_a(0)
+        place_a(1)
+        quantise_w2(0, 0)
+        quantise_w2(1, 0)
+        quantise_w2(0, 1)
+        quantise_w2(1, 1)
+        w3_raw[1] = load_rows(w3, PASS, 0, "w3_raw", 3)
+        eph[1, 0] = load_rows(ephem, PASS, 0, "eph", 4)
+        eph[1, 1] = load_rows(ephem, PASS, PASS, "eph", 5)
+        [place_a(s) for s in range(2, 8)]
+        [second_product(s) for s in range(5)]
+        quantise_w3(0)
+        quantise_w3(1)
+        place_b(0)
+        second_product(5)
+        place_b(1)
+        second_product(6)
+        place_b(2)
+        second_product(7)
+        place_b(3)
+        place_b(4)
+        turn_back(0, 0)
+        make_z(0, 0, z_tile())
+        turn_back(0, 1)
+        place_b(5)
+        place_b(6)
+        place_b(7)
+        make_z(0, 1, keep.tile([P, PASS, 4], BF16, name="z_bf01", tag="pre0", align_bytes=64))
+        turn_back(1, 0)
+        make_z(1, 0, z_tile())
+        turn_back(1, 1)
+        make_z(1, 1, z_tile())
+        [last_product(h, nb) for h in range(2) for nb in range(4)]

@@ -21,7 +21,11 @@ ALU = mybir.AluOpType
 P = 128
 PASS = 512
 SLICES = H // P
-PAGES_B = 3
+PAGES_B = 2
+AHEAD = 4
+LEAD = 3
+RUN = 4
+NCOS = 8
 ROUND_BIAS = 0.0
 
 
@@ -36,24 +40,21 @@ def tile_list_lightcurve_slot_scores_kernel(
         ring = ctx.enter_context(tc.tile_pool(name="ring", bufs=2))
         psum = ctx.enter_context(tc.psum_pool(name="psum", bufs=2))
 
-        def wide(shape, dtype, name, slot):
-            return keep.tile(shape, dtype, name=name, tag=f"wide{slot}", align_bytes=64)
+        def shared(place, shape, dtype, name):
+            return keep.tile(shape, dtype, name=name, tag=place, align_bytes=64)
 
-        def stage(shape, dtype, name):
-            return ring.tile(shape, dtype, name=name, tag="stage", bufs=2, align_bytes=64)
-
-        def feat(name):
-            return ring.tile([P, S], F32, name=name, tag="feat", bufs=SLICES)
+        def work_bank(shape, name):
+            return psum.tile(shape, F32, name=name, tag="work", bufs=4)
 
         def load_list(src, name):
             t = lists.tile([P, S // 16], U16, name=name)
             nc.sync.dma_start(t[:], src)
             return t
 
-        def load_scales_side_by_side(src, width, name, clear, queue):
-            t = keep.tile([P, 2 * width], U8, name=name, tag=name, align_bytes=64)
+        def load_scales_side_by_side(src, width, name, queue):
+            t = shared(name, [P, 2 * width], U8, name)
             view = t[:].bitcast(I32)
-            clear.memset(view, 0)
+            nc.vector.memset(view, 0)
             rows = src.bitcast(I32)
             for q in range(4):
                 queue.dma_start(
@@ -62,186 +63,185 @@ def tile_list_lightcurve_slot_scores_kernel(
                 )
             return t
 
-        tab_s = load_scales_side_by_side(tab_scales, T, "tab_s", nc.vector, nc.scalar)
-        list1 = load_list(offs, "list1")
-        list3 = load_list(offs3, "list3")
-        list2 = load_list(offs2, "list2")
-        list4 = load_list(offs4, "list4")
-        tab_w = []
-        for a in range(2):
-            t = wide([P, T], U32, f"tab_w{a}", a)
-            nc.sync.dma_start(t[:].bitcast(I32), tab_words[a].rearrange("p t i -> p (t i)").bitcast(I32))
-            tab_w.append(t)
-        tab2_w = wide([P, 2 * TG], U32, "tab2_w", 2)
-        nc.sync.dma_start(
-            tab2_w[:].bitcast(I32).rearrange("p (a t) -> p a t", a=2),
-            tab2_words.rearrange("a p t i -> p a (t i)").bitcast(I32),
-        )
-        w1_w = keep.tile([P, 2, 2 * H], U8, name="w1_w", align_bytes=64)
-        nc.sync.dma_start(
-            w1_w[:].rearrange("p a n -> p (a n)").bitcast(I32).rearrange("p (a n) -> p a n", a=2),
-            w1_words.bitcast(I32).rearrange("a p n -> p a n"),
-        )
-        w1_s = load_scales_side_by_side(w1_scales, H, "w1_s", nc.gpsimd, nc.gpsimd)
-        vec_rows = keep.tile([P, P], F32, name="vec_rows", tag="vec_rows", align_bytes=64)
-        nc.vector.memset(vec_rows[:], 0.0)
-        nc.gpsimd.dma_start(vec_rows[0:SLICES, :], base.rearrange("(s p) -> s p", p=P))
-        nc.gpsimd.dma_start(vec_rows[32 : 32 + SLICES, :], amp.rearrange("(s p) -> s p", p=P))
-        wg1_sb = keep.tile([P, S], F32, name="wg1_sb")
-        nc.sync.dma_start(wg1_sb[:], wg1)
-
-
-        tab2_s = keep.tile([P, TG], U8, name="tab2_s", align_bytes=64)
-        nc.vector.memset(tab2_s[:].bitcast(I32), 0)
-        for q in range(4):
-            nc.gpsimd.dma_start(
-                tab2_s[:].bitcast(I32)[32 * q : 32 * q + 8, :],
-                tab2_scales.bitcast(I32)[:, 4 * q : 4 * q + 4, :],
-            )
-
-        ident = keep.tile([P, P], F32, name="ident")
-        make_identity(nc, ident[:])
-        vec_ps = psum.tile([P, PASS], F32, name="vec_ps", tag="work", bufs=4)
-        nc.tensor.transpose(vec_ps[:, 0:P], vec_rows[:], ident[:])
-        vec = keep.tile([P, 64], F32, name="vec")
-        nc.scalar.copy(vec[:], vec_ps[:, 0:64])
-
-        page_a = [keep.tile([P, T2], F32, name=f"page_a{i}") for i in range(SLICES)]
-        page_b = [keep.tile([P, T2], F32, name=f"page_b{i}") for i in range(PAGES_B)]
-        for page in page_a + page_b:
-            nc.gpsimd.memset(page[:], 0.0)
-
-        v_w, v_s = [], []
-        for a in range(2):
-            s_t = keep.tile([P, S], U8, name=f"v_s{a}", align_bytes=64)
-            nc.vector.tensor_copy(s_t[:], tab_s[:, a * T : (a + 1) * T].indirect(list1[:]))
-            v_s.append(s_t)
-        v_both = keep.tile([P, 2, S], U32, name="v_both", tag="tab_s", align_bytes=64)
-        for a in range(2):
-            nc.vector.tensor_copy(v_both[:, a, :], tab_w[a][:].indirect(list1[:]))
-            v_w.append(v_both[:, a, :])
-
-
-        h1_raw = {}
-
-        def first_product(s):
-            acc = psum.tile([P, S], F32, name="acc", tag="mx")
-            for a in range(2):
-                nc.tensor.matmul_mx(
-                    out=acc[:],
-                    lhsT=w1_w[:, a, 2 * P * s : 2 * P * (s + 1)].bitcast(FP4X4),
-                    lhsT_scale=w1_s[:, a * H + P * s : a * H + P * (s + 1)],
-                    rhs=v_w[a][:].bitcast(FP8X4),
-                    rhs_scale=v_s[a][:],
-                    start=(a == 0),
-                    stop=(a == 1),
-                )
-            t = feat("h1_raw")
-            nc.scalar.copy(t[:], acc[:])
-            h1_raw[s] = t
-
-        def place_a(s):
-            h1 = keep.tile([P, S], F32, name="h1", tag=f"h1_{s}" if s < 2 else f"pre{min(s - 2, 2 + s % 2)}", align_bytes=64)
-            nc.vector.tensor_scalar(h1[:], h1_raw[s][:], vec[:, s : s + 1], None, ALU.max)
-            nc.vector.tensor_tensor(page_a[s][:].indirect(list3[:]), h1[:], wg1_sb[:], ALU.mult)
-
-        def load_rows(src, row0, col0, name, slot):
-            t = wide([P, 4, PASS], F32, name, slot)
+        def load_rows(src, row0, col0, name, place):
+            t = shared(place, [P, 4, PASS], F32, name)
             nc.sync.dma_start(
                 t[:], src[row0 : row0 + PASS, col0 : col0 + PASS].rearrange("(p j) c -> p j c", j=4)
             )
             return t
 
-        def quantise_weight(raw, name, grouped):
-            nc.scalar.copy(
-                grouped[:].rearrange("p (c i) t -> p c t i", i=4),
-                raw[:].rearrange("p t (c i) -> p c t i", i=4),
-            )
-            codes = keep.tile([P, PASS], U32, name=name + "_w", align_bytes=64)
-            scales = keep.tile([P, PASS], U8, name=name + "_s", align_bytes=64)
-            nc.vector.quantize_mx(
-                out=codes[:].bitcast(FP8X4), scales=scales[:], in_=grouped[:].rearrange("p c t -> p (c t)")
-            )
-            return codes, scales
+        ident = keep.tile([P, P], F32, name="ident")
+        make_identity(nc, ident[:])
 
-        for s in range(SLICES):
-            first_product(s)
-
-        v2_w = []
-        v2_s = keep.tile([P, S], U8, name="v2_s", tag="vec_rows", align_bytes=64)
-        v2_both = wide([P, 2, S], U32, "v2_both", 1)
+        list1 = load_list(offs, "list1")
+        list3 = load_list(offs3, "list3")
+        list2 = load_list(offs2, "list2")
+        list4 = load_list(offs4, "list4")
+        tab_s = load_scales_side_by_side(tab_scales, T, "tab_s", nc.scalar)
+        vec_rows = keep.tile([P, P], F32, name="vec_rows")
+        nc.vector.memset(vec_rows[:], 0.0)
+        nc.scalar.dma_start(vec_rows[0:SLICES, :], base.rearrange("(s p) -> s p", p=P))
+        nc.scalar.dma_start(vec_rows[32 : 32 + SLICES, :], amp.rearrange("(s p) -> s p", p=P))
+        tab_w = []
         for a in range(2):
-            nc.vector.tensor_copy(v2_both[:, a, :], tab2_w[:, a * TG : (a + 1) * TG].indirect(list2[:]))
-            v2_w.append(v2_both[:, a, :])
+            t = shared(f"wide{a}", [P, T], U32, f"tab_w{a}")
+            nc.sync.dma_start(t[:].bitcast(I32), tab_words[a].rearrange("p t i -> p (t i)").bitcast(I32))
+            tab_w.append(t)
+        w1_w = keep.tile([P, 2, 2 * H], U8, name="w1_w", align_bytes=64)
+        nc.sync.dma_start(
+            w1_w[:].rearrange("p a n -> p (a n)").bitcast(I32).rearrange("p (a n) -> p a n", a=2),
+            w1_words.bitcast(I32).rearrange("a p n -> p a n"),
+        )
+        tab2_w = shared("wide2", [P, 2 * TG], U32, "tab2_w")
+        nc.sync.dma_start(
+            tab2_w[:].bitcast(I32).rearrange("p (a t) -> p a t", a=2),
+            tab2_words.rearrange("a p t i -> p a (t i)").bitcast(I32),
+        )
+        wg1_sb = keep.tile([P, S], F32, name="wg1_sb")
+        nc.sync.dma_start(wg1_sb[:], wg1)
+        w1_s = load_scales_side_by_side(w1_scales, H, "w1_s", nc.gpsimd)
+        tab2_s = shared("tab2_s", [P, TG], U8, "tab2_s")
+        nc.vector.memset(tab2_s[:].bitcast(I32), 0)
+        for q in range(4):
+            nc.sync.dma_start(
+                tab2_s[:].bitcast(I32)[32 * q : 32 * q + 8, :],
+                tab2_scales.bitcast(I32)[:, 4 * q : 4 * q + 4, :],
+            )
+        w2_raw = {(a, 0): load_rows(w2, a * PASS, 0, "w2_raw", f"wide{3 + a}") for a in range(2)}
+        wg2_sb = keep.tile([P, S], F32, name="wg2_sb")
+        nc.sync.dma_start(wg2_sb[:], wg2)
+
+        vec_ps = work_bank([P, P], "vec_ps")
+        nc.tensor.transpose(vec_ps[:], vec_rows[:], ident[:])
+        vec = keep.tile([P, 64], F32, name="vec")
+        nc.scalar.copy(vec[:], vec_ps[:, 0:64])
+
+        pages = {}
+
+        def clear_page(i):
+            pages[i] = shared(f"page{i}", [P, T2], F32, f"page{i}")
+            nc.gpsimd.memset(pages[i][:], 0.0)
+
+        for i in (0, 1):
+            clear_page(i)
+
+        v_s = []
+        for a in range(2):
+            s_t = keep.tile([P, S], U8, name=f"v_s{a}", align_bytes=64)
+            nc.vector.tensor_copy(s_t[:], tab_s[:, a * T : (a + 1) * T].indirect(list1[:]))
+            v_s.append(s_t)
+        v_w = shared("tab_s", [P, 2, S], U32, "v_w")
+        for a in range(2):
+            nc.vector.tensor_copy(v_w[:, a, :], tab_w[a][:].indirect(list1[:]))
+        v2_w = shared("wide1", [P, 2, S], U32, "v2_w")
+        for a in range(2):
+            nc.vector.tensor_copy(v2_w[:, a, :], tab2_w[:, a * TG : (a + 1) * TG].indirect(list2[:]))
+        v2_s = shared("v2_s", [P, S], U8, "v2_s")
         nc.vector.tensor_copy(v2_s[:], tab2_s[:].indirect(list2[:]))
 
-        w2_raw = {}
-        for half in range(2):
+        w2_raw[0, 1] = load_rows(w2, 0, PASS, "w2_raw", "wide0")
+        w2_raw[1, 1] = load_rows(w2, PASS, PASS, "w2_raw", "wide5")
+        w3_raw = {0: load_rows(w3, 0, 0, "w3_raw", "wide2")}
+        eph = {(0, half): load_rows(ephem, 0, half * PASS, "eph", f"wide{6 + half}") for half in range(2)}
+
+        h1_raw = {}
+
+        def first_product(s):
+            acc = work_bank([P, S], "acc")
             for a in range(2):
-                w2_raw[a, half] = load_rows(w2, a * PASS, half * PASS, "w2_raw", ((3, 4), (0, 5))[half][a])
-            if half == 0:
-                wg2_sb = keep.tile([P, S], F32, name="wg2_sb")
-                nc.sync.dma_start(wg2_sb[:], wg2)
-        w3_raw = {0: load_rows(w3, 0, 0, "w3_raw", 2)}
-        eph = {}
-        for b, half, slot in ((0, 0, 6), (0, 1, 7)):
-            eph[b, half] = load_rows(ephem, b * PASS, half * PASS, "eph", slot)
-
-
-        w2_q = {}
-        cosine = {}
-
-        def quantise_w2(a, half):
-            w2_q[a, half] = quantise_weight(
-                w2_raw[a, half], f"w2_{a}{half}",
-                keep.tile([P, PASS, 4], BF16, name="grouped", tag=f"pre{2 * half + a}", align_bytes=64),
-            )
-
-        def second_product(s):
-            half, c0 = s // 4, (s % 4) * P
-            acc = psum.tile([P, S], F32, name="acc", tag="mx")
-            for a in range(2):
-                codes, scales = w2_q[a, half]
                 nc.tensor.matmul_mx(
                     out=acc[:],
-                    lhsT=codes[:, c0 : c0 + P].bitcast(FP8X4),
-                    lhsT_scale=scales[:, c0 : c0 + P],
-                    rhs=v2_w[a][:].bitcast(FP8X4),
-                    rhs_scale=v2_s[4 * a : P, :],
+                    lhsT=w1_w[:, a, 2 * P * s : 2 * P * (s + 1)].bitcast(FP4X4),
+                    lhsT_scale=w1_s[:, a * H + P * s : a * H + P * (s + 1)],
+                    rhs=v_w[:, a, :].bitcast(FP8X4),
+                    rhs_scale=v_s[a][:],
                     start=(a == 0),
                     stop=(a == 1),
                 )
-            size = ring.tile([P, S], F32, name="size")
-            nc.scalar.activation(size[:], acc[:], ACT.Abs)
-            turns = ring.tile([P, S], U32, name="turns")
-            nc.scalar.activation(turns[:], size[:], ACT.Copy, bias=ROUND_BIAS, scale=1.0 / (2.0 * math.pi))
-            whole = ring.tile([P, S], F32, name="whole")
-            nc.scalar.activation(whole[:], turns[:], ACT.Copy, bias=0.0, scale=-2.0 * math.pi)
-            angle = psum.tile([P, 4, P], F32, name="angle", tag="work", bufs=4)
-            for blk in range(4):
-                cols = slice(blk * P, (blk + 1) * P)
-                nc.tensor.matmul(angle[:, blk, :], size[:, cols], ident[:], start=True, stop=False, is_transpose=True)
-                nc.tensor.matmul(angle[:, blk, :], whole[:, cols], ident[:], start=False, stop=True, is_transpose=True)
-            folded = ring.tile([P, 4, P], F32, name="folded")
-            nc.scalar.activation(folded[:], angle[:], ACT.Abs)
-            upright = psum.tile([P, S], F32, name="upright", tag="work", bufs=4)
-            for blk in range(4):
-                nc.tensor.transpose(upright[:, blk * P : (blk + 1) * P], folded[:, blk, :], ident[:])
-            c = keep.tile([P, S], F32, name="cos_last", tag="pre0", align_bytes=64) if s == SLICES - 1 else feat("cos_t")
-            nc.scalar.activation(c[:], upright[:], ACT.Sin, bias=math.pi / 2.0, scale=-1.0)
-            nc.scalar.activation(c[:], c[:], ACT.Copy, bias=0.0, scale=vec[:, 32 + s : 33 + s])
-            cosine[s] = c
+            h1_raw[s] = shared(f"page{s + 2}" if s + 2 < SLICES else f"h1_raw{s}", [P, S], F32, "h1_raw")
+            nc.scalar.copy(h1_raw[s][:], acc[:])
 
-        turned = {}
+        def place_a(s, h1):
+            nc.vector.tensor_scalar(h1, h1_raw[s][:], vec[:, s : s + 1], None, ALU.max)
+            if s + 2 < SLICES:
+                clear_page(s + 2)
+            nc.vector.tensor_tensor(pages[s][:].indirect(list3[:]), h1, wg1_sb[:], ALU.mult)
+
+        def interleaved(ap):
+            return ap.rearrange("p (c i) t -> p c t i", i=RUN)
+
+        def by_runs(ap):
+            return ap.rearrange("p t (c i) -> p c t i", i=RUN)
+
+        def quantise(grouped, name):
+            codes = keep.tile([P, PASS], U32, name=name + "_w", align_bytes=64)
+            scales = keep.tile([P, PASS], U8, name=name + "_s", align_bytes=64)
+            nc.vector.quantize_mx(
+                out=codes[:].bitcast(FP8X4), scales=scales[:], in_=grouped.rearrange("p c t -> p (c t)")
+            )
+            return codes, scales
+
+        def quantise_weight(raw, name, grouped):
+            nc.scalar.copy(
+                grouped.rearrange("p (c i) t -> p c t i", i=4), raw[:].rearrange("p t (c i) -> p c t i", i=4)
+            )
+            return quantise(grouped, name)
+
+        def grouped_at(place):
+            t = shared(place, [P, PASS, 4], BF16, "grouped")
+            return t[:]
+
+        w2_q, w3_q, z_q = {}, {}, {}
+        cosine, turned, back = {}, {}, {}
+
+        def h1_at(place):
+            t = shared(place, [P, S], F32, "h1")
+            return t[:]
+
+        turns = {}
+
+        def second_product(half):
+            cosine[half] = shared(f"cos{half}", [P, 4, S], F32, "cosine")
+            turns[half] = shared(f"turns{half}", [P, 4, S], U32, "turns")
+            for sl in range(4):
+                acc = psum.tile([P, S], F32, name="acc", tag="mx")
+                for a in range(2):
+                    codes, scales = w2_q[a, half]
+                    nc.tensor.matmul_mx(
+                        out=acc[:],
+                        lhsT=codes[:, sl * P : (sl + 1) * P].bitcast(FP8X4),
+                        lhsT_scale=scales[:, sl * P : (sl + 1) * P],
+                        rhs=v2_w[:, a, :].bitcast(FP8X4),
+                        rhs_scale=v2_s[4 * a : P, :],
+                        start=(a == 0),
+                        stop=(a == 1),
+                    )
+                nc.scalar.activation(cosine[half][:, sl, :], acc[:], ACT.Abs)
+                nc.scalar.activation(
+                    turns[half][:, sl, :], cosine[half][:, sl, :], ACT.Copy, bias=ROUND_BIAS, scale=1.0 / (2.0 * math.pi)
+                )
+
+        def reduce_angles(half):
+            size = cosine[half][:].rearrange("p s j -> p (s j)")
+            nc.vector.scalar_tensor_tensor(
+                size, turns[half][:].rearrange("p s j -> p (s j)").bitcast(I32), -2.0 * math.pi, size, ALU.mult, ALU.add
+            )
+
+        def take_cosine(s, place):
+            c = cosine[s // 4][:, s % 4, :]
+            nc.scalar.activation(c, c, ACT.Abs)
+            sine = shared(place, [P, S], F32, "sine")
+            nc.scalar.activation(sine[:], c, ACT.Sin, bias=math.pi / 2.0, scale=-1.0)
+            nc.scalar.activation(c, sine[:], ACT.Copy, bias=0.0, scale=vec[:, 32 + s : 33 + s])
 
         def place_b(s):
-            pa, pb = page_a[s], page_b[s % PAGES_B]
-            nc.vector.tensor_tensor(pb[:].indirect(list4[:]), cosine[s][:], wg2_sb[:], ALU.mult)
+            pa, pb = pages[s], pages[SLICES + s % PAGES_B]
+            nc.vector.tensor_tensor(pb[:].indirect(list4[:]), cosine[s // 4][:, s % 4, :], wg2_sb[:], ALU.mult)
             b, sl = s // 4, s % 4
             for half in range(2):
                 if sl == 0:
-                    turned[b, half] = wide([P, 4, 4, P], F32, "turned", ((0, 2), (3, 1))[b][half])
-                bank = psum.tile([P, 4, P], F32, name="sum_ps", tag="work", bufs=4)
+                    turned[b, half] = shared(f"wide{((0, 2), (3, 1))[b][half]}", [P, 4, 4, P], F32, "turned")
+                bank = work_bank([P, 4, P], "sum_ps")
                 for k, page in enumerate((pa, pb)):
                     for blk in range(4):
                         cols = slice(half * PASS + blk * P, half * PASS + (blk + 1) * P)
@@ -254,10 +254,6 @@ def tile_list_lightcurve_slot_scores_kernel(
                     bank[:].rearrange("p blk (q t) -> p blk t q", t=4),
                 )
 
-        z_q = {}
-
-        back = {}
-
         def turn_back(b, half):
             for blk in range(4):
                 bank = psum.tile([P, 4, P], F32, name="back_ps", tag=("turn", "mx")[blk % 2])
@@ -265,32 +261,17 @@ def tile_list_lightcurve_slot_scores_kernel(
                     nc.tensor.transpose(bank[:, t, :], turned[b, half][:, blk, t, :], ident[:])
                 back[b, half, blk] = bank
 
-        def make_z(b, half, z_bf):
+        def make_z(b, half, place):
+            z_bf = shared(place, [P, PASS, 4], BF16, "z_bf")
             for blk in range(4):
-                bank = back[b, half, blk]
+                cols = slice(blk * P, (blk + 1) * P)
                 nc.vector.tensor_tensor(
-                    z_bf[:, blk * P : (blk + 1) * P, :].rearrange("p (c i) t -> p c t i", i=4),
-                    bank[:].rearrange("p t (c i) -> p c t i", i=4),
-                    eph[b, half][:, :, blk * P : (blk + 1) * P].rearrange("p t (c i) -> p c t i", i=4),
-                    ALU.max,
+                    interleaved(z_bf[:, cols, :]), by_runs(back[b, half, blk][:]), by_runs(eph[b, half][:, :, cols]), ALU.max
                 )
-            codes = keep.tile([P, PASS], U32, name=f"z_w{b}{half}", align_bytes=64)
-            scales = keep.tile([P, PASS], U8, name=f"z_s{b}{half}", align_bytes=64)
-            nc.vector.quantize_mx(
-                out=codes[:].bitcast(FP8X4), scales=scales[:], in_=z_bf[:].rearrange("p c t -> p (c t)")
-            )
-            z_q[b, half] = (codes, scales)
-
-        def z_tile():
-            return ring.tile([P, PASS, 4], BF16, name="z_bf", align_bytes=64)
-
-        w3_q = {}
-
-        def quantise_w3(b):
-            w3_q[b] = quantise_weight(w3_raw[b], f"w3_{b}", z_tile())
+            z_q[b, half] = quantise(z_bf[:], f"z{b}{half}")
 
         def last_product(half, nb):
-            acc = psum.tile([P, PASS], F32, name="acc", tag="work", bufs=4)
+            acc = work_bank([P, PASS], "acc")
             for b in range(2):
                 nc.tensor.matmul_mx(
                     out=acc[:],
@@ -303,40 +284,51 @@ def tile_list_lightcurve_slot_scores_kernel(
                 )
             th = ring.tile([P, PASS], F32, name="th", bufs=4)
             nc.scalar.activation(th[:], acc[:], ACT.Tanh)
-            res = feat("res")
+            res = ring.tile([P, PASS], F32, name="res", bufs=8)
             nc.vector.tensor_tensor(res[:], acc[:], th[:], ALU.mult)
             nc.sync.dma_start(out[nb * P : (nb + 1) * P, half * PASS : (half + 1) * PASS], res[:])
 
-        place_a(0)
-        place_a(1)
-        quantise_w2(0, 0)
-        quantise_w2(1, 0)
-        quantise_w2(0, 1)
-        quantise_w2(1, 1)
-        w3_raw[1] = load_rows(w3, PASS, 0, "w3_raw", 3)
-        eph[1, 0] = load_rows(ephem, PASS, 0, "eph", 4)
-        eph[1, 1] = load_rows(ephem, PASS, PASS, "eph", 5)
-        [place_a(s) for s in range(2, 8)]
-        [second_product(s) for s in range(5)]
-        quantise_w3(0)
-        quantise_w3(1)
-        place_b(0)
-        second_product(5)
-        place_b(1)
-        second_product(6)
-        place_b(2)
-        second_product(7)
-        place_b(3)
-        place_b(4)
-        turn_back(0, 0)
-        make_z(0, 0, z_tile())
-        turn_back(0, 1)
-        place_b(5)
-        place_b(6)
-        place_b(7)
-        make_z(0, 1, keep.tile([P, PASS, 4], BF16, name="z_bf01", tag="pre0", align_bytes=64))
+        for s in range(3):
+            first_product(s)
+        place_a(0, h1_at("h1_0"))
+        for a in range(2):
+            w2_q[a, 0] = quantise_weight(w2_raw[a, 0], f"w2_{a}0", grouped_at(f"pre{a}"))
+            place_a(1 + a, h1_at(f"pre{a}"))
+        for s in range(3, SLICES):
+            first_product(s)
+        for a in range(2):
+            w2_q[a, 1] = quantise_weight(w2_raw[a, 1], f"w2_{a}1", grouped_at(f"pre{2 + a}"))
+        w3_raw[1] = load_rows(w3, PASS, 0, "w3_raw", "wide3")
+        eph[1, 0] = load_rows(ephem, PASS, 0, "eph", "wide4")
+        eph[1, 1] = load_rows(ephem, PASS, PASS, "eph", "wide5")
+        second_product(0)
+        place_a(3, h1_at("pre2"))
+        reduce_angles(0)
+        place_a(4, h1_at("turns0"))
+        place_a(5, h1_at("pre3"))
+        second_product(1)
+        reduce_angles(1)
+        place_a(6, h1_at("turns1"))
+        place_a(7, h1_at("turns1"))
+        for s in range(SLICES):
+            hold = s - 4
+            take_cosine(s, f"page{SLICES + hold}" if 0 <= hold < PAGES_B else f"sine{s % 2}")
+            if 0 <= hold < PAGES_B:
+                clear_page(SLICES + hold)
+        for b in range(2):
+            w3_q[b] = quantise_weight(w3_raw[b], f"w3_{b}", grouped_at(f"pre{b}"))
+        for s in range(SLICES):
+            place_b(s)
+            if s == 4:
+                turn_back(0, 0)
+                make_z(0, 0, "pre2")
+            if s == 6:
+                turn_back(0, 1)
+        make_z(0, 1, "cos1")
         turn_back(1, 0)
-        make_z(1, 0, z_tile())
+        make_z(1, 0, "pre3")
         turn_back(1, 1)
-        make_z(1, 1, z_tile())
-        [last_product(h, nb) for h in range(2) for nb in range(4)]
+        make_z(1, 1, "pre0")
+        for half in range(2):
+            for nb in range(4):
+                last_product(half, nb)

@@ -120,9 +120,9 @@ def tile_list_lightcurve_slot_scores_kernel(
 
         def clear_page(i):
             pages[i] = shared(f"page{i}", [P, T2], F32, f"page{i}")
-            nc.gpsimd.memset(pages[i][:], 0.0)
+            nc.vector.memset(pages[i][:], 0.0)
 
-        for i in (0, 1):
+        for i in range(SLICES):
             clear_page(i)
 
         v_s = []
@@ -139,12 +139,12 @@ def tile_list_lightcurve_slot_scores_kernel(
         v2_s = shared("v2_s", [P, S], U8, "v2_s")
         nc.vector.tensor_copy(v2_s[:], tab2_s[:].indirect(list2[:]))
 
-        w2_raw[0, 1] = load_rows(w2, 0, PASS, "w2_raw", "wide0")
-        w2_raw[1, 1] = load_rows(w2, PASS, PASS, "w2_raw", "wide5")
+        w2_raw[0, 1] = load_rows(w2, 0, PASS, "w2_raw", "wide5")
+        w2_raw[1, 1] = load_rows(w2, PASS, PASS, "w2_raw", "wide0")
         w3_raw = {0: load_rows(w3, 0, 0, "w3_raw", "wide2")}
         eph = {(0, half): load_rows(ephem, 0, half * PASS, "eph", f"wide{6 + half}") for half in range(2)}
 
-        h1_raw = {}
+        h1_raw, floored = {}, {}
 
         def first_product(s):
             acc = work_bank([P, S], "acc")
@@ -158,14 +158,15 @@ def tile_list_lightcurve_slot_scores_kernel(
                     start=(a == 0),
                     stop=(a == 1),
                 )
-            h1_raw[s] = shared(f"page{s + 2}" if s + 2 < SLICES else f"h1_raw{s}", [P, S], F32, "h1_raw")
+            h1_raw[s] = shared(f"h1_raw{s}", [P, S], F32, "h1_raw")
             nc.scalar.copy(h1_raw[s][:], acc[:])
 
-        def place_a(s, h1):
+        def apply_floor(s, h1):
             nc.vector.tensor_scalar(h1, h1_raw[s][:], vec[:, s : s + 1], None, ALU.max)
-            if s + 2 < SLICES:
-                clear_page(s + 2)
-            nc.vector.tensor_tensor(pages[s][:].indirect(list3[:]), h1, wg1_sb[:], ALU.mult)
+            floored[s] = h1
+
+        def place_a(s):
+            nc.vector.tensor_tensor(pages[s][:].indirect(list3[:]), floored[s], wg1_sb[:], ALU.mult)
 
         def interleaved(ap):
             return ap.rearrange("p (c i) t -> p c t i", i=RUN)
@@ -181,11 +182,10 @@ def tile_list_lightcurve_slot_scores_kernel(
             )
             return codes, scales
 
-        def quantise_weight(raw, name, grouped):
+        def round_weight(raw, grouped):
             nc.scalar.copy(
                 grouped.rearrange("p (c i) t -> p c t i", i=4), raw[:].rearrange("p t (c i) -> p c t i", i=4)
             )
-            return quantise(grouped, name)
 
         def grouped_at(place):
             t = shared(place, [P, PASS, 4], BF16, "grouped")
@@ -282,41 +282,51 @@ def tile_list_lightcurve_slot_scores_kernel(
                     start=(b == 0),
                     stop=(b == 1),
                 )
-            th = ring.tile([P, PASS], F32, name="th", bufs=4)
+            th = ring.tile([P, PASS], F32, name="th", bufs=3)
             nc.scalar.activation(th[:], acc[:], ACT.Tanh)
-            res = ring.tile([P, PASS], F32, name="res", bufs=8)
-            nc.vector.tensor_tensor(res[:], acc[:], th[:], ALU.mult)
-            nc.sync.dma_start(out[nb * P : (nb + 1) * P, half * PASS : (half + 1) * PASS], res[:])
+            res = results[half][:, nb, :]
+            nc.vector.tensor_tensor(res, acc[:], th[:], ALU.mult)
+            nc.sync.dma_start(out[nb * P : (nb + 1) * P, half * PASS : (half + 1) * PASS], res)
 
         for s in range(3):
             first_product(s)
-        place_a(0, h1_at("h1_0"))
+        apply_floor(0, h1_at("h1_0"))
+        place_a(0)
         for a in range(2):
-            w2_q[a, 0] = quantise_weight(w2_raw[a, 0], f"w2_{a}0", grouped_at(f"pre{a}"))
-            place_a(1 + a, h1_at(f"pre{a}"))
+            grouped = grouped_at(f"pre{a}")
+            round_weight(w2_raw[a, 0], grouped)
+            apply_floor(1 + a, h1_at(f"wide{3 + a}"))
+            w2_q[a, 0] = quantise(grouped, f"w2_{a}0")
+            place_a(1 + a)
         for s in range(3, SLICES):
             first_product(s)
         for a in range(2):
-            w2_q[a, 1] = quantise_weight(w2_raw[a, 1], f"w2_{a}1", grouped_at(f"pre{2 + a}"))
+            grouped = grouped_at(f"pre{2 + a}")
+            round_weight(w2_raw[a, 1], grouped)
+            if a == 0:
+                apply_floor(3, h1_at("wide5"))
+            w2_q[a, 1] = quantise(grouped, f"w2_{a}1")
         w3_raw[1] = load_rows(w3, PASS, 0, "w3_raw", "wide3")
         eph[1, 0] = load_rows(ephem, PASS, 0, "eph", "wide4")
+        place_a(3)
         eph[1, 1] = load_rows(ephem, PASS, PASS, "eph", "wide5")
-        second_product(0)
-        place_a(3, h1_at("pre2"))
-        reduce_angles(0)
-        place_a(4, h1_at("turns0"))
-        place_a(5, h1_at("pre3"))
-        second_product(1)
-        reduce_angles(1)
-        place_a(6, h1_at("turns1"))
-        place_a(7, h1_at("turns1"))
+        for half in range(2):
+            second_product(half)
+            reduce_angles(half)
+            pair = shared(f"turns{half}", [P, 2, S], F32, "pair")
+            for i in range(2):
+                apply_floor(4 + 2 * half + i, pair[:, i, :])
+            for i in range(2):
+                place_a(4 + 2 * half + i)
         for s in range(SLICES):
             hold = s - 4
             take_cosine(s, f"page{SLICES + hold}" if 0 <= hold < PAGES_B else f"sine{s % 2}")
             if 0 <= hold < PAGES_B:
                 clear_page(SLICES + hold)
         for b in range(2):
-            w3_q[b] = quantise_weight(w3_raw[b], f"w3_{b}", grouped_at(f"pre{b}"))
+            grouped = grouped_at(f"pre{b}")
+            round_weight(w3_raw[b], grouped)
+            w3_q[b] = quantise(grouped, f"w3_{b}")
         for s in range(SLICES):
             place_b(s)
             if s == 4:
@@ -329,6 +339,7 @@ def tile_list_lightcurve_slot_scores_kernel(
         make_z(1, 0, "pre3")
         turn_back(1, 1)
         make_z(1, 1, "pre0")
+        results = [shared(f"turns{half}", [P, 4, PASS], F32, "results") for half in range(2)]
         for half in range(2):
             for nb in range(4):
                 last_product(half, nb)

@@ -25,6 +25,7 @@ PAGES_B = 2
 AHEAD = 4
 LEAD = 3
 RUN = 4
+CLEARED_FIRST = 5
 NCOS = 8
 ROUND_BIAS = 0.0
 
@@ -63,6 +64,12 @@ def tile_list_lightcurve_slot_scores_kernel(
                 )
             return t
 
+        def load_by_slice(vector, name, queue):
+            t = keep.tile([P, SLICES], F32, name=name)
+            with nc.allow_non_contiguous_dma(reason="one value of each slice of 128 rows to each partition"):
+                queue.dma_start(t[:], vector.rearrange("(s p) -> p s", p=P))
+            return t
+
         def load_rows(src, row0, col0, name, place):
             t = shared(place, [P, 4, PASS], F32, name)
             nc.sync.dma_start(
@@ -77,53 +84,49 @@ def tile_list_lightcurve_slot_scores_kernel(
         list3 = load_list(offs3, "list3")
         list2 = load_list(offs2, "list2")
         list4 = load_list(offs4, "list4")
+        base_sb = load_by_slice(base, "base_sb", nc.scalar)
         tab_s = load_scales_side_by_side(tab_scales, T, "tab_s", nc.scalar)
-        vec_rows = keep.tile([P, P], F32, name="vec_rows")
-        nc.vector.memset(vec_rows[:], 0.0)
-        nc.scalar.dma_start(vec_rows[0:SLICES, :], base.rearrange("(s p) -> s p", p=P))
-        nc.scalar.dma_start(vec_rows[32 : 32 + SLICES, :], amp.rearrange("(s p) -> s p", p=P))
         tab_w = []
         for a in range(2):
             t = shared(f"wide{a}", [P, T], U32, f"tab_w{a}")
             nc.sync.dma_start(t[:].bitcast(I32), tab_words[a].rearrange("p t i -> p (t i)").bitcast(I32))
             tab_w.append(t)
-        w1_w = keep.tile([P, 2, 2 * H], U8, name="w1_w", align_bytes=64)
-        nc.sync.dma_start(
-            w1_w[:].rearrange("p a n -> p (a n)").bitcast(I32).rearrange("p (a n) -> p a n", a=2),
-            w1_words.bitcast(I32).rearrange("a p n -> p a n"),
-        )
         tab2_w = shared("wide2", [P, 2 * TG], U32, "tab2_w")
         nc.sync.dma_start(
             tab2_w[:].bitcast(I32).rearrange("p (a t) -> p a t", a=2),
             tab2_words.rearrange("a p t i -> p a (t i)").bitcast(I32),
         )
+        w1_w = keep.tile([P, 2, 2 * H], U8, name="w1_w", align_bytes=64)
+        nc.sync.dma_start(
+            w1_w[:].rearrange("p a n -> p (a n)").bitcast(I32).rearrange("p (a n) -> p a n", a=2),
+            w1_words.bitcast(I32).rearrange("a p n -> p a n"),
+        )
         wg1_sb = keep.tile([P, S], F32, name="wg1_sb")
         nc.sync.dma_start(wg1_sb[:], wg1)
-        w1_s = load_scales_side_by_side(w1_scales, H, "w1_s", nc.gpsimd)
+        w1_s = load_scales_side_by_side(w1_scales, H, "w1_s", nc.scalar)
+        w2_raw = {(0, 0): load_rows(w2, 0, 0, "w2_raw", "wide3")}
         tab2_s = shared("tab2_s", [P, TG], U8, "tab2_s")
         nc.vector.memset(tab2_s[:].bitcast(I32), 0)
         for q in range(4):
-            nc.sync.dma_start(
+            nc.scalar.dma_start(
                 tab2_s[:].bitcast(I32)[32 * q : 32 * q + 8, :],
                 tab2_scales.bitcast(I32)[:, 4 * q : 4 * q + 4, :],
             )
-        w2_raw = {(a, 0): load_rows(w2, a * PASS, 0, "w2_raw", f"wide{3 + a}") for a in range(2)}
+        w2_raw[1, 0] = load_rows(w2, PASS, 0, "w2_raw", "wide4")
         wg2_sb = keep.tile([P, S], F32, name="wg2_sb")
         nc.sync.dma_start(wg2_sb[:], wg2)
 
-        vec_ps = work_bank([P, P], "vec_ps")
-        nc.tensor.transpose(vec_ps[:], vec_rows[:], ident[:])
-        vec = keep.tile([P, 64], F32, name="vec")
-        nc.scalar.copy(vec[:], vec_ps[:, 0:64])
+
+        amp_sb = load_by_slice(amp, "amp_sb", nc.sync)
 
         pages = {}
 
-        def clear_page(i):
+        def clear_page(i, engine):
             pages[i] = shared(f"page{i}", [P, T2], F32, f"page{i}")
-            nc.vector.memset(pages[i][:], 0.0)
+            engine.memset(pages[i][:].bitcast(I32), 0)
 
-        for i in range(SLICES):
-            clear_page(i)
+        for i in range(CLEARED_FIRST):
+            clear_page(i, nc.vector)
 
         v_s = []
         for a in range(2):
@@ -158,14 +161,19 @@ def tile_list_lightcurve_slot_scores_kernel(
                     start=(a == 0),
                     stop=(a == 1),
                 )
-            h1_raw[s] = shared(f"h1_raw{s}", [P, S], F32, "h1_raw")
+            h1_raw[s] = shared(f"page{CLEARED_FIRST + s}" if CLEARED_FIRST + s < SLICES else f"h1_raw{s}", [P, S], F32, "h1_raw")
             nc.scalar.copy(h1_raw[s][:], acc[:])
 
         def apply_floor(s, h1):
-            nc.vector.tensor_scalar(h1, h1_raw[s][:], vec[:, s : s + 1], None, ALU.max)
+            nc.vector.tensor_scalar(h1, h1_raw[s][:], base_sb[:, s : s + 1], None, ALU.max)
             floored[s] = h1
 
+        def clear_behind(s):
+            if CLEARED_FIRST + s < SLICES:
+                clear_page(CLEARED_FIRST + s, nc.gpsimd)
+
         def place_a(s):
+            clear_behind(s)
             nc.vector.tensor_tensor(pages[s][:].indirect(list3[:]), floored[s], wg1_sb[:], ALU.mult)
 
         def interleaved(ap):
@@ -232,7 +240,7 @@ def tile_list_lightcurve_slot_scores_kernel(
             nc.scalar.activation(c, c, ACT.Abs)
             sine = shared(place, [P, S], F32, "sine")
             nc.scalar.activation(sine[:], c, ACT.Sin, bias=math.pi / 2.0, scale=-1.0)
-            nc.scalar.activation(c, sine[:], ACT.Copy, bias=0.0, scale=vec[:, 32 + s : 33 + s])
+            nc.scalar.activation(c, sine[:], ACT.Copy, bias=0.0, scale=amp_sb[:, s : s + 1])
 
         def place_b(s):
             pa, pb = pages[s], pages[SLICES + s % PAGES_B]
@@ -322,7 +330,7 @@ def tile_list_lightcurve_slot_scores_kernel(
             hold = s - 4
             take_cosine(s, f"page{SLICES + hold}" if 0 <= hold < PAGES_B else f"sine{s % 2}")
             if 0 <= hold < PAGES_B:
-                clear_page(SLICES + hold)
+                clear_page(SLICES + hold, nc.gpsimd)
         for b in range(2):
             grouped = grouped_at(f"pre{b}")
             round_weight(w3_raw[b], grouped)

import math
from contextlib import ExitStack

import concourse.mybir as mybir
from concourse.masks import make_identity

K, H, N, T, TG, S, T2 = 1024, 1024, 512, 2048, 1024, 512, 1024
FLOPS = 2 * K * H * S * 2 + 2 * H * N * T2

F32 = mybir.dt.float32
BF16 = mybir.dt.bfloat16
I32 = mybir.dt.int32
U32 = mybir.dt.uint32
U16 = mybir.dt.uint16
U8 = mybir.dt.uint8
FP8X4 = mybir.dt.float8_e4m3fn_x4
FP4X4 = mybir.dt.float4_e2m1fn_x4
ACT = mybir.ActivationFunctionType
ALU = mybir.AluOpType

P = 128
PASS = 512
SLICES = H // P
PAGES_B = 2
AHEAD = 4
LEAD = 3
RUN = 4
CLEARED_FIRST = 5
NCOS = 8
ROUND_BIAS = 0.0


def tile_list_lightcurve_slot_scores_kernel(
    tc, tab_words, tab_scales, tab2_words, tab2_scales, offs, offs2, offs3, offs4,
    w1_words, w1_scales, base, w2, amp, wg1, wg2, ephem, w3, out,
):
    nc = tc.nc
    with ExitStack() as ctx:
        lists = ctx.enter_context(tc.tile_pool(name="lists", bufs=1))
        keep = ctx.enter_context(tc.tile_pool(name="keep", bufs=1))
        ring = ctx.enter_context(tc.tile_pool(name="ring", bufs=2))
        psum = ctx.enter_context(tc.psum_pool(name="psum", bufs=2))

        def shared(place, shape, dtype, name):
            return keep.tile(shape, dtype, name=name, tag=place, align_bytes=64)

        def work_bank(shape, name):
            return psum.tile(shape, F32, name=name, tag="work", bufs=4)

        def load_list(src, name):
            t = lists.tile([P, S // 16], U16, name=name)
            nc.sync.dma_start(t[:], src)
            return t

        def load_scales_side_by_side(src, width, name, queue):
            t = shared(name, [P, 2 * width], U8, name)
            view = t[:].bitcast(I32)
            nc.vector.memset(view, 0)
            rows = src.bitcast(I32)
            for q in range(4):
                queue.dma_start(
                    view[32 * q : 32 * q + 4, :].rearrange("r (a n) -> r a n", a=2),
                    rows[:, 4 * q : 4 * q + 4, :].rearrange("a r n -> r a n"),
                )
            return t

        def load_by_slice(vector, name, queue):
            t = keep.tile([P, SLICES], F32, name=name)
            with nc.allow_non_contiguous_dma(reason="one value of each slice of 128 rows to each partition"):
                queue.dma_start(t[:], vector.rearrange("(s p) -> p s", p=P))
            return t

        def load_rows(src, row0, col0, name, place):
            t = shared(place, [P, 4, PASS], F32, name)
            nc.sync.dma_start(
                t[:], src[row0 : row0 + PASS, col0 : col0 + PASS].rearrange("(p j) c -> p j c", j=4)
            )
            return t

        ident = keep.tile([P, P], F32, name="ident")
        make_identity(nc, ident[:])

        list1 = load_list(offs, "list1")
        list3 = load_list(offs3, "list3")
        list2 = load_list(offs2, "list2")
        list4 = load_list(offs4, "list4")
        base_sb = load_by_slice(base, "base_sb", nc.scalar)
        tab_s = load_scales_side_by_side(tab_scales, T, "tab_s", nc.scalar)
        tab_w = []
        for a in range(2):
            t = shared(f"wide{a}", [P, T], U32, f"tab_w{a}")
            nc.sync.dma_start(t[:].bitcast(I32), tab_words[a].rearrange("p t i -> p (t i)").bitcast(I32))
            tab_w.append(t)
        tab2_w = shared("wide2", [P, 2 * TG], U32, "tab2_w")
        nc.sync.dma_start(
            tab2_w[:].bitcast(I32).rearrange("p (a t) -> p a t", a=2),
            tab2_words.rearrange("a p t i -> p a (t i)").bitcast(I32),
        )
        w1_w = keep.tile([P, 2, 2 * H], U8, name="w1_w", align_bytes=64)
        nc.sync.dma_start(
            w1_w[:].rearrange("p a n -> p (a n)").bitcast(I32).rearrange("p (a n) -> p a n", a=2),
            w1_words.bitcast(I32).rearrange("a p n -> p a n"),
        )
        wg1_sb = keep.tile([P, S], F32, name="wg1_sb")
        nc.sync.dma_start(wg1_sb[:], wg1)
        w1_s = load_scales_side_by_side(w1_scales, H, "w1_s", nc.scalar)
        w2_raw = {(0, 0): load_rows(w2, 0, 0, "w2_raw", "wide3")}
        tab2_s = shared("tab2_s", [P, TG], U8, "tab2_s")
        nc.vector.memset(tab2_s[:].bitcast(I32), 0)
        for q in range(4):
            nc.scalar.dma_start(
                tab2_s[:].bitcast(I32)[32 * q : 32 * q + 8, :],
                tab2_scales.bitcast(I32)[:, 4 * q : 4 * q + 4, :],
            )
        w2_raw[1, 0] = load_rows(w2, PASS, 0, "w2_raw", "wide4")
        wg2_sb = keep.tile([P, S], F32, name="wg2_sb")
        nc.sync.dma_start(wg2_sb[:], wg2)


        amp_sb = load_by_slice(amp, "amp_sb", nc.sync)

        pages = {}

        def clear_page(i, engine):
            pages[i] = shared(f"page{i}", [P, T2], F32, f"page{i}")
            engine.memset(pages[i][:].bitcast(I32), 0)

        for i in range(CLEARED_FIRST):
            clear_page(i, nc.vector)

        v_s = []
        for a in range(2):
            s_t = keep.tile([P, S], U8, name=f"v_s{a}", align_bytes=64)
            nc.vector.tensor_copy(s_t[:], tab_s[:, a * T : (a + 1) * T].indirect(list1[:]))
            v_s.append(s_t)
        v_w = shared("tab_s", [P, 2, S], U32, "v_w")
        for a in range(2):
            nc.vector.tensor_copy(v_w[:, a, :], tab_w[a][:].indirect(list1[:]))
        v2_w = shared("wide1", [P, 2, S], U32, "v2_w")
        for a in range(2):
            nc.vector.tensor_copy(v2_w[:, a, :], tab2_w[:, a * TG : (a + 1) * TG].indirect(list2[:]))
        v2_s = shared("v2_s", [P, S], U8, "v2_s")
        nc.vector.tensor_copy(v2_s[:], tab2_s[:].indirect(list2[:]))

        w2_raw[0, 1] = load_rows(w2, 0, PASS, "w2_raw", "wide5")
        w2_raw[1, 1] = load_rows(w2, PASS, PASS, "w2_raw", "wide0")
        w3_raw = {0: load_rows(w3, 0, 0, "w3_raw", "wide2")}
        eph = {(0, half): load_rows(ephem, 0, half * PASS, "eph", f"wide{6 + half}") for half in range(2)}

        h1_raw, floored = {}, {}

        def first_product(s):
            acc = work_bank([P, S], "acc")
            for a in range(2):
                nc.tensor.matmul_mx(
                    out=acc[:],
                    lhsT=w1_w[:, a, 2 * P * s : 2 * P * (s + 1)].bitcast(FP4X4),
                    lhsT_scale=w1_s[:, a * H + P * s : a * H + P * (s + 1)],
                    rhs=v_w[:, a, :].bitcast(FP8X4),
                    rhs_scale=v_s[a][:],
                    start=(a == 0),
                    stop=(a == 1),
                )
            h1_raw[s] = shared(f"page{CLEARED_FIRST + s}" if CLEARED_FIRST + s < SLICES else f"h1_raw{s}", [P, S], F32, "h1_raw")
            nc.scalar.copy(h1_raw[s][:], acc[:])

        def apply_floor(s, h1):
            nc.vector.tensor_scalar(h1, h1_raw[s][:], base_sb[:, s : s + 1], None, ALU.max)
            floored[s] = h1

        def clear_behind(s):
            if CLEARED_FIRST + s < SLICES:
                clear_page(CLEARED_FIRST + s, nc.gpsimd)

        def place_a(s):
            clear_behind(s)
            nc.vector.tensor_tensor(pages[s][:].indirect(list3[:]), floored[s], wg1_sb[:], ALU.mult)

        def interleaved(ap):
            return ap.rearrange("p (c i) t -> p c t i", i=RUN)

        def by_runs(ap):
            return ap.rearrange("p t (c i) -> p c t i", i=RUN)

        def quantise(grouped, name):
            codes = keep.tile([P, PASS], U32, name=name + "_w", align_bytes=64)
            scales = keep.tile([P, PASS], U8, name=name + "_s", align_bytes=64)
            nc.vector.quantize_mx(
                out=codes[:].bitcast(FP8X4), scales=scales[:], in_=grouped.rearrange("p c t -> p (c t)")
            )
            return codes, scales

        def round_weight(raw, grouped):
            nc.scalar.copy(
                grouped.rearrange("p (c i) t -> p c t i", i=4), raw[:].rearrange("p t (c i) -> p c t i", i=4)
            )

        def grouped_at(place):
            t = shared(place, [P, PASS, 4], BF16, "grouped")
            return t[:]

        w2_q, w3_q, z_q = {}, {}, {}
        cosine, turned, back = {}, {}, {}

        def h1_at(place):
            t = shared(place, [P, S], F32, "h1")
            return t[:]

        turns = {}

        def second_product(half):
            cosine[half] = shared(f"cos{half}", [P, 4, S], F32, "cosine")
            turns[half] = shared(f"turns{half}", [P, 4, S], U32, "turns")
            for sl in range(4):
                acc = psum.tile([P, S], F32, name="acc", tag="mx")
                for a in range(2):
                    codes, scales = w2_q[a, half]
                    nc.tensor.matmul_mx(
                        out=acc[:],
                        lhsT=codes[:, sl * P : (sl + 1) * P].bitcast(FP8X4),
                        lhsT_scale=scales[:, sl * P : (sl + 1) * P],
                        rhs=v2_w[:, a, :].bitcast(FP8X4),
                        rhs_scale=v2_s[4 * a : P, :],
                        start=(a == 0),
                        stop=(a == 1),
                    )
                nc.scalar.activation(cosine[half][:, sl, :], acc[:], ACT.Abs)
                nc.scalar.activation(
                    turns[half][:, sl, :], cosine[half][:, sl, :], ACT.Copy, bias=ROUND_BIAS, scale=1.0 / (2.0 * math.pi)
                )

        def reduce_angles(half):
            size = cosine[half][:].rearrange("p s j -> p (s j)")
            nc.vector.scalar_tensor_tensor(
                size, turns[half][:].rearrange("p s j -> p (s j)").bitcast(I32), -2.0 * math.pi, size, ALU.mult, ALU.add
            )

        def take_cosine(s, place):
            c = cosine[s // 4][:, s % 4, :]
            nc.scalar.activation(c, c, ACT.Abs)
            sine = shared(place, [P, S], F32, "sine")
            nc.scalar.activation(sine[:], c, ACT.Sin, bias=math.pi / 2.0, scale=-1.0)
            nc.scalar.activation(c, sine[:], ACT.Copy, bias=0.0, scale=amp_sb[:, s : s + 1])

        def place_b(s):
            pa, pb = pages[s], pages[SLICES + s % PAGES_B]
            nc.vector.tensor_tensor(pb[:].indirect(list4[:]), cosine[s // 4][:, s % 4, :], wg2_sb[:], ALU.mult)
            b, sl = s // 4, s % 4
            for half in range(2):
                if sl == 0:
                    turned[b, half] = shared(f"wide{((0, 2), (3, 1))[b][half]}", [P, 4, 4, P], F32, "turned")
                bank = work_bank([P, 4, P], "sum_ps")
                for k, page in enumerate((pa, pb)):
                    for blk in range(4):
                        cols = slice(half * PASS + blk * P, half * PASS + (blk + 1) * P)
                        nc.tensor.matmul(
                            bank[:, blk, :], page[:, cols], ident[:],
                            start=(k == 0 and blk == 0), stop=(k == 1 and blk == 3), is_transpose=True,
                        )
                nc.scalar.copy(
                    turned[b, half][:, :, :, 32 * sl : 32 * (sl + 1)],
                    bank[:].rearrange("p blk (q t) -> p blk t q", t=4),
                )

        def turn_back(b, half):
            for blk in range(4):
                bank = psum.tile([P, 4, P], F32, name="back_ps", tag=("turn", "mx")[blk % 2])
                for t in range(4):
                    nc.tensor.transpose(bank[:, t, :], turned[b, half][:, blk, t, :], ident[:])
                back[b, half, blk] = bank

        def make_z(b, half, place):
            z_bf = shared(place, [P, PASS, 4], BF16, "z_bf")
            for blk in range(4):
                cols = slice(blk * P, (blk + 1) * P)
                nc.vector.tensor_tensor(
                    interleaved(z_bf[:, cols, :]), by_runs(back[b, half, blk][:]), by_runs(eph[b, half][:, :, cols]), ALU.max
                )
            z_q[b, half] = quantise(z_bf[:], f"z{b}{half}")

        def last_product(half, nb):
            acc = work_bank([P, PASS], "acc")
            for b in range(2):
                nc.tensor.matmul_mx(
                    out=acc[:],
                    lhsT=w3_q[b][0][:, nb * P : (nb + 1) * P].bitcast(FP8X4),
                    lhsT_scale=w3_q[b][1][:, nb * P : (nb + 1) * P],
                    rhs=z_q[b, half][0][:].bitcast(FP8X4),
                    rhs_scale=z_q[b, half][1][:],
                    start=(b == 0),
                    stop=(b == 1),
                )
            th = ring.tile([P, PASS], F32, name="th", bufs=3)
            nc.scalar.activation(th[:], acc[:], ACT.Tanh)
            res = results[half][:, nb, :]
            nc.vector.tensor_tensor(res, acc[:], th[:], ALU.mult)
            nc.sync.dma_start(out[nb * P : (nb + 1) * P, half * PASS : (half + 1) * PASS], res)

        for s in range(3):
            first_product(s)
        apply_floor(0, h1_at("h1_0"))
        place_a(0)
        for a in range(2):
            grouped = grouped_at(f"pre{a}")
            round_weight(w2_raw[a, 0], grouped)
            apply_floor(1 + a, h1_at(f"wide{3 + a}"))
            w2_q[a, 0] = quantise(grouped, f"w2_{a}0")
            place_a(1 + a)
        for s in range(3, SLICES):
            first_product(s)
        for a in range(2):
            grouped = grouped_at(f"pre{2 + a}")
            round_weight(w2_raw[a, 1], grouped)
            if a == 0:
                apply_floor(3, h1_at("wide5"))
            w2_q[a, 1] = quantise(grouped, f"w2_{a}1")
        w3_raw[1] = load_rows(w3, PASS, 0, "w3_raw", "wide3")
        eph[1, 0] = load_rows(ephem, PASS, 0, "eph", "wide4")
        place_a(3)
        eph[1, 1] = load_rows(ephem, PASS, PASS, "eph", "wide5")
        for half in range(2):
            second_product(half)
            reduce_angles(half)
            pair = shared(f"turns{half}", [P, 2, S], F32, "pair")
            for i in range(2):
                apply_floor(4 + 2 * half + i, pair[:, i, :])
            for i in range(2):
                place_a(4 + 2 * half + i)
        for s in range(SLICES):
            hold = s - 4
            take_cosine(s, f"page{SLICES + hold}" if 0 <= hold < PAGES_B else f"sine{s % 2}")
            if 0 <= hold < PAGES_B:
                clear_page(SLICES + hold, nc.gpsimd)
        for b in range(2):
            grouped = grouped_at(f"pre{b}")
            round_weight(w3_raw[b], grouped)
            w3_q[b] = quantise(grouped, f"w3_{b}")
        for s in range(SLICES):
            place_b(s)
            if s == 4:
                turn_back(0, 0)
                make_z(0, 0, "pre2")
            if s == 6:
                turn_back(0, 1)
        make_z(0, 1, "cos1")
        turn_back(1, 0)
        make_z(1, 0, "pre3")
        turn_back(1, 1)
        make_z(1, 1, "pre0")
        results = [shared(f"turns{half}", [P, 4, PASS], F32, "results") for half in range(2)]
        for half in range(2):
            for nb in range(4):
                last_product(half, nb)
